import numpy as np
import ml_dtypes


def mxq(x, axis, fmt="e4m3"):
    dtype, down = {"e4m3": (ml_dtypes.float8_e4m3fn, 7), "e5m2": (ml_dtypes.float8_e5m2, 14)}[fmt]
    v = np.moveaxis(np.asarray(x, np.float32).astype(ml_dtypes.bfloat16).astype(np.float64), axis, -1)
    blocks = v.reshape(v.shape[:-1] + (-1, 32))
    amax = np.abs(blocks).max(-1, keepdims=True)
    byte = np.maximum(np.where(amax > 0, np.frexp(amax)[1] - 1 + 127, 0) - down, 1)
    scale = np.exp2(byte - 127.0)
    codes = (blocks / scale).astype(np.float32).astype(dtype).astype(np.float64)
    return np.moveaxis((codes * scale).reshape(v.shape), -1, axis)


WIDE = False


def mx_kscale(k):
    if not WIDE:
        return np.ones(k)
    levels = np.array([10, -10, 5, -5, 0])
    if k % 512:
        return np.exp2(np.random.permutation(np.resize(levels, k // 32))).repeat(32)
    a = np.empty((k // 512, 16))
    for p in range(k // 512):
        a[p, :8] = np.random.permutation(np.resize(levels, 8))
        for g in range(8):
            far = levels[np.abs(levels - a[p, g]) >= 10]
            a[p, g + 8] = far[np.random.randint(len(far))]
    return np.exp2(a.ravel()).repeat(32)


def f64(x):
    return np.asarray(x).astype(np.float64)


def striped(idx):
    return np.tile(idx.reshape(-1, 16).T, (8, 1)).astype(np.uint16)


def unstriped(offs):
    return offs[:16].T.reshape(-1).astype(np.int64)


def striped8(idx):
    return np.concatenate([x.reshape(-1, 16).T for x in idx]).astype(np.uint16)


def runs(offs, k):
    lists = np.stack([offs[16 * r : 16 * r + 16].T.reshape(-1) for r in range(8)]).astype(np.int64)
    return lists[np.arange(k) % 512 // 64]


def pack_weight(w):
    k, n = w.shape
    w = f64(np.asarray(w, np.float32).astype(ml_dtypes.bfloat16)).reshape(k // 32, 32, n)
    amax = np.abs(w).max(1)
    byte = np.clip(np.where(amax > 0, np.frexp(amax)[1] - 1 + 127 - 7, 1), 1, 254)
    scaled = (w * np.exp2(127.0 - byte)[:, None, :]).reshape(k, n).astype(np.float32)
    words = np.ascontiguousarray(scaled.reshape(k // 512, 128, 4, n).transpose(0, 1, 3, 2)).astype(ml_dtypes.float8_e4m3fn).view(np.uint8)
    return words, np.ascontiguousarray(byte.astype(np.uint8).reshape(k // 512, 16, n))


def unpack_weight(words, scales):
    g, p, n, _ = words.shape
    vals = np.ascontiguousarray(words).view(ml_dtypes.float8_e4m3fn).astype(np.float64) * np.repeat(np.exp2(scales.astype(np.float64) - 127.0), 8, axis=1)[..., None]
    return vals.transpose(0, 1, 3, 2).reshape(g * 512, n)


def sigmoid(v):
    return 1.0 / (1.0 + np.exp(-np.maximum(v, -700.0)))


K, T, S, N, H, G, W = 512, 2048, 512, 512, 512, 2048, 1024


def setup_inputs():
    n = np.random.standard_normal
    s = mx_kscale(K)[:, None]
    u = mx_kscale(S)
    packed_xT = pack_weight(n((K, T)) * s)
    packed_dT = pack_weight(n((K, G)) / s)
    return {
        "x_words": packed_xT[0],
        "x_scales": packed_xT[1],
        "w1": (n((K, H)) / np.sqrt(K) / s).astype(np.float32),
        "d_words": packed_dT[0],
        "d_scales": packed_dT[1],
        "gn": (np.random.uniform(0.5, 1.5, (H, 1)) * u[:, None]).astype(np.float32),
        "w2": (n((H, N)) / np.sqrt(H) / u[:, None]).astype(np.float32),
        "offs": striped(np.random.permutation(T)[:S]),
        "k1": striped8(np.random.randint(0, G, (8, H))),
        "two": striped(np.random.permutation(T)[:S]),
        "n1": striped8(np.stack([np.random.permutation(S) for _ in range(8)])),
        "n2": striped8(np.stack([np.random.permutation(S) for _ in range(8)])),
        "n3": striped8(np.stack([np.random.permutation(S) for _ in range(8)])),
        "n4": striped8(np.stack([np.random.permutation(S) for _ in range(8)])),
        "n5": striped(np.random.randint(0, S, W)),
    }


def reference(x_words, x_scales, w1, d_words, d_scales, gn, w2, offs, k1, two, n1, n2, n3, n4, n5):
    xq = unpack_weight(x_words, x_scales)[:, unstriped(offs)]
    y = mxq(f64(w1), 0, "e4m3").T @ xq
    d_k1 = unpack_weight(d_words, d_scales)[np.arange(K)[:, None], runs(k1, K)]
    x_two = unpack_weight(x_words, x_scales)[:, unstriped(two)]
    d = 0.0625 * (d_k1.T @ x_two)
    z = f64(gn) * (np.maximum(y[np.arange(H)[:, None], runs(n1, H)] + d[np.arange(H)[:, None], runs(n3, H)], y[np.arange(H)[:, None], runs(n2, H)] + d[np.arange(H)[:, None], runs(n4, H)]))
    h = mxq(f64(w2), 0, "e4m3").T @ mxq(z, 0, "e4m3")
    mb = h[:, unstriped(n5)]
    mn = mb.reshape(N, S, 2).min(axis=2)
    mx = mb.reshape(N, S, 2).max(axis=2)
    return (h - mn) * sigmoid(mx)

@@ -1,0 +1,185 @@
+from contextlib import ExitStack
+
+import concourse.mybir as mybir
+
+F32 = mybir.dt.float32
+BF16 = mybir.dt.bfloat16
+I32 = mybir.dt.int32
+U32 = mybir.dt.uint32
+U16 = mybir.dt.uint16
+U8 = mybir.dt.uint8
+FP8X4 = mybir.dt.float8_e4m3fn_x4
+ALU = mybir.AluOpType
+ACT = mybir.ActivationFunctionType
+
+P = 128
+PACK = 4
+T = 2048
+S = 512
+HALF = 256
+SPARE = 32
+FLOPS = 3 * 2 * 512 * 512 * 512
+
+
+def tile_picked_twkeypathbghard_none_p_kernel(tc, x_words, x_scales, w1, d_words, d_scales, gn, w2, offs, k1, two, n1, n2, n3, n4, n5, out):
+    nc = tc.nc
+    with ExitStack() as ctx:
+        lists = ctx.enter_context(tc.tile_pool(name="lists", bufs=1))
+        keep = ctx.enter_context(tc.tile_pool(name="keep", bufs=1))
+        work = ctx.enter_context(tc.tile_pool(name="work", bufs=3))
+        psum = ctx.enter_context(tc.psum_pool(name="psum", bufs=1))
+
+        def load_list(src, name):
+            tile = lists.tile(list(src.shape), U16, name=name)
+            nc.sync.dma_start(tile[:], src)
+            return tile
+
+        def load_words(src, name):
+            tile = keep.tile([P, T], I32, name=name)
+            nc.sync.dma_start(tile[:], src[0].rearrange("p n t -> p (n t)").bitcast(I32))
+            return tile
+
+        def load_weight(src, name):
+            tile = keep.tile([P, PACK, src.shape[1]], F32, name=name)
+            nc.sync.dma_start(tile[:], src.rearrange("(p j) c -> p j c", j=PACK))
+            return tile
+
+        d_bytes = keep.tile([P, T], U8, name="d_bytes")
+        x_bytes = keep.tile([P, T], U8, name="x_bytes")
+        dk_scales = keep.tile([P, S], U8, name="dk_scales", align_bytes=64)
+        nc.gpsimd.memset(dk_scales[:].bitcast(I32), 0)
+        h_rows = [keep.tile([P, S + SPARE], F32, name=f"h_rows{m}") for m in range(PACK)]
+        for m in range(PACK):
+            nc.gpsimd.memset(h_rows[m][:, S:], 0.0)
+
+        k1_sb = load_list(k1, "k1_sb")
+        nc.sync.dma_start(d_bytes[:].bitcast(I32), d_scales[0].bitcast(I32).unsqueeze(1).broadcast_to([16, 8, T // 4]))
+        offs_sb = load_list(offs, "offs_sb")
+        for q in range(4):
+            rows = x_scales[0, 4 * q : 4 * q + 4, :].bitcast(I32)
+            nc.sync.dma_start(x_bytes[32 * q : 32 * (q + 1), :].bitcast(I32), rows.unsqueeze(0).broadcast_to([8, 4, T // 4]))
+        w1_raw = [load_weight(w1[:, :HALF], "w1_raw0")]
+        two_sb = load_list(two, "two_sb")
+        w1_raw.append(load_weight(w1[:, HALF:], "w1_raw1"))
+        x_table = load_words(x_words, "x_table")
+        n1_sb = load_list(n1, "n1_sb")
+        n2_sb = load_list(n2, "n2_sb")
+        d_table = load_words(d_words, "d_table")
+        n3_sb = load_list(n3, "n3_sb")
+        n4_sb = load_list(n4, "n4_sb")
+        gain = keep.tile([P, PACK], F32, name="gain")
+        nc.sync.dma_start(gain[:], gn.rearrange("(p t) o -> p (t o)", t=PACK))
+        w2_raw = load_weight(w2, "w2_raw")
+        n5_sb = load_list(n5, "n5_sb")
+
+        def gather_bytes(table, offsets, name):
+            picked = keep.tile([P, S], U8, name=name, align_bytes=64)
+            nc.vector.tensor_copy(picked[:], table[:].indirect(offsets[:]))
+            return picked
+
+        def gather_words(table, offsets, name):
+            picked = keep.tile([P, S], U32, name=name, align_bytes=64)
+            nc.vector.tensor_copy(picked[:], table[:].bitcast(U32).indirect(offsets[:]))
+            return picked
+
+        def deal(src, dtype, name):
+            dealt = keep.tile([P, S], dtype, name=name, align_bytes=64)
+            nc.vector.tensor_copy(dealt[:].rearrange("p (t m) -> p m t", t=PACK), src[:].rearrange("p (m t) -> p m t", t=PACK))
+            return dealt
+
+        def quantize(values, name):
+            width = values.shape[1] // PACK
+            codes = keep.tile([P, width], U32, name=name + "_codes", align_bytes=64)
+            scales = keep.tile([P, width], U8, name=name + "_scales", align_bytes=64)
+            nc.vector.quantize_mx(out=codes[:].bitcast(FP8X4), scales=scales[:], in_=values)
+            return codes, scales
+
+        def product(acc, w_codes, w_scales, t, codes, scales):
+            cols = slice(P * t, P * (t + 1))
+            nc.tensor.matmul_mx(acc, lhsT=w_codes[:, cols].bitcast(FP8X4), lhsT_scale=w_scales[:, cols],
+                                rhs=codes[:].bitcast(FP8X4), rhs_scale=scales[:], start=True, stop=True)
+
+        dk_bytes = gather_bytes(d_bytes, k1_sb, "dk_bytes")
+        dk_dealt = deal(dk_bytes, U8, "dk_dealt")
+        for i in range(4):
+            nc.gpsimd.dma_start(dk_scales[i:P:32, :].bitcast(I32), dk_dealt[8 * i : P : 32, :].bitcast(I32))
+        xo_scales = gather_bytes(x_bytes, offs_sb, "xo_scales")
+        xt_scales = gather_bytes(x_bytes, two_sb, "xt_scales")
+
+        w1_bf = keep.tile([P, PACK * S], BF16, name="w1_bf", align_bytes=64)
+        w1_dealt = w1_bf[:].rearrange("p (t m j) -> p m j t", t=PACK, j=PACK)
+        for c in range(2):
+            nc.scalar.copy(w1_dealt[:, 64 * c : 64 * (c + 1)], w1_raw[c][:].rearrange("p j (m t) -> p m j t", t=PACK))
+        w1_codes, w1_scales = quantize(w1_bf[:], "w1")
+        xo_codes = gather_words(x_table, offs_sb, "xo_codes")
+        y_acc = [psum.tile([P, S], F32, name=f"y_acc{t}", tag=f"bank{t}") for t in range(PACK)]
+        for t in range(PACK):
+            product(y_acc[t][:], w1_codes, w1_scales, t, xo_codes, xo_scales)
+
+        xt_codes = gather_words(x_table, two_sb, "xt_codes")
+        dk_words = gather_words(d_table, k1_sb, "dk_words")
+        dk_codes = deal(dk_words, U32, "dk_codes")
+        d_acc = [psum.tile([P, S], F32, name=f"d_acc{t}", tag=f"bank{PACK + t}") for t in range(PACK)]
+        for t in range(PACK):
+            product(d_acc[t][:], dk_codes, dk_scales, t, xt_codes, xt_scales)
+
+        y_rows = [keep.tile([P, S], F32, name=f"y_rows{t}") for t in range(PACK)]
+        d_rows = [keep.tile([P, S], F32, name=f"d_rows{t}") for t in range(PACK)]
+        w2_bf = keep.tile([P, PACK * S], BF16, name="w2_bf", align_bytes=64)
+        h_acc = [psum.tile([P, S], F32, name=f"h_acc{m}", tag=f"bank{m}") for m in range(PACK)]
+        gain_b = gain[:].unsqueeze(1).unsqueeze(3).broadcast_to([P, HALF // 4, PACK, 4])
+
+        for c in range(S // HALF):
+            entries = slice(c * HALF // 16, (c + 1) * HALF // 16)
+            cols = slice(c * HALF, (c + 1) * HALF)
+            larger = keep.tile([P, PACK, HALF], F32, name=f"larger{c}")
+            for t in range(PACK):
+                if c == 0:
+                    nc.scalar.copy(y_rows[t][:], y_acc[t][:])
+                    if t == 0:
+                        nc.vector.tensor_scalar(d_rows[t][:], d_acc[t][:], 0.0625, None, ALU.mult)
+                    else:
+                        nc.scalar.activation(d_rows[t][:], d_acc[t][:], ACT.Copy, scale=0.0625)
+                sums = []
+                for y_list, d_list in ((n1_sb, n3_sb), (n2_sb, n4_sb)):
+                    y_picked = work.tile([P, HALF], F32, name="y_picked", bufs=16)
+                    nc.scalar.activation(y_picked[:], y_rows[t][:].indirect(y_list[:, entries]), ACT.Copy)
+                    total = work.tile([P, HALF], F32, name="total", bufs=4)
+                    nc.vector.tensor_tensor(total[:], d_rows[t][:].indirect(d_list[:, entries]), y_picked[:], ALU.add)
+                    sums.append(total)
+                nc.vector.tensor_tensor(larger[:, t, :], sums[0][:], sums[1][:], ALU.max)
+            if c == 0:
+                nc.scalar.copy(w2_bf[:].rearrange("p (c i j) -> p c j i", i=4, j=PACK), w2_raw[:].rearrange("p j (c i) -> p c j i", i=4))
+                w2_codes, w2_scales = quantize(w2_bf[:], "w2")
+            z_bf = keep.tile([P, PACK * HALF], BF16, name=f"z_bf{c}", align_bytes=64)
+            nc.vector.tensor_tensor(z_bf[:].rearrange("p (c i t) -> p c t i", i=4, t=PACK),
+                                    larger[:].rearrange("p t (c i) -> p c t i", i=4), gain_b, ALU.mult)
+            z_codes, z_scales = quantize(z_bf[:], f"z{c}")
+            for m in range(PACK):
+                product(h_acc[m][:, cols], w2_codes, w2_scales, m, z_codes, z_scales)
+                if c == 1 and m == 0:
+                    nc.vector.tensor_copy(h_rows[m][:, cols], h_acc[m][:, cols])
+                else:
+                    nc.scalar.copy(h_rows[m][:, cols], h_acc[m][:, cols])
+
+        for m in range(PACK):
+            for c in range(S // HALF):
+                cols = slice(c * HALF, (c + 1) * HALF)
+                window = h_rows[m][:].indirect(n5_sb[:, c * 2 * HALF // 16 : (c + 1) * 2 * HALF // 16])
+                members = work.tile([P, HALF, 2], F32, name="members", bufs=4)
+                flat = members[:].rearrange("p c e -> p (c e)")
+                if (m, c) in ((0, 0), (2, 0)):
+                    nc.vector.tensor_copy(flat, window)
+                else:
+                    nc.scalar.activation(flat, window, ACT.Copy)
+                hi = work.tile([P, HALF], F32, name="hi")
+                lo = work.tile([P, HALF], F32, name="lo")
+                nc.vector.tensor_tensor(hi[:], members[:, :, 0], members[:, :, 1], ALU.max)
+                nc.vector.tensor_tensor(lo[:], members[:, :, 0], members[:, :, 1], ALU.min)
+                gate = work.tile([P, HALF], F32, name="gate")
+                nc.scalar.activation(gate[:], hi[:], ACT.Sigmoid)
+                diff = work.tile([P, HALF], F32, name="diff")
+                nc.vector.tensor_tensor(diff[:], h_rows[m][:, cols], lo[:], ALU.subtract)
+                result = work.tile([P, HALF], F32, name="result", bufs=8)
+                nc.vector.tensor_tensor(result[:], diff[:], gate[:], ALU.mult)
+                nc.sync.dma_start(out[P * m : P * (m + 1), cols], result[:])

@@ -39,41 +39,43 @@ def tile_picked_twkeypathbghard_none_p_kernel(tc, x_words, x_scales, w1, d_words
             nc.sync.dma_start(tile[:], src[0].rearrange("p n t -> p (n t)").bitcast(I32))
             return tile
 
-        def load_weight(src, name):
-            tile = keep.tile([P, PACK, src.shape[1]], F32, name=name)
+        def load_weight(src, name, tag):
+            tile = keep.tile([P, PACK, src.shape[1]], F32, name=name, tag=tag, align_bytes=64)
             nc.sync.dma_start(tile[:], src.rearrange("(p j) c -> p j c", j=PACK))
             return tile
 
         d_bytes = keep.tile([P, T], U8, name="d_bytes")
         x_bytes = keep.tile([P, T], U8, name="x_bytes")
+        nc.gpsimd.memset(d_bytes[:].bitcast(I32), 0)
         dk_scales = keep.tile([P, S], U8, name="dk_scales", align_bytes=64)
         nc.gpsimd.memset(dk_scales[:].bitcast(I32), 0)
         h_rows = [keep.tile([P, S + SPARE], F32, name=f"h_rows{m}") for m in range(PACK)]
         for m in range(PACK):
             nc.gpsimd.memset(h_rows[m][:, S:], 0.0)
 
-        k1_sb = load_list(k1, "k1_sb")
-        nc.sync.dma_start(d_bytes[:].bitcast(I32), d_scales[0].bitcast(I32).unsqueeze(1).broadcast_to([16, 8, T // 4]))
+        warm = keep.tile([P, 8], F32, name="warm")
+        nc.scalar.activation(warm[:], h_rows[0][:, S : S + 8], ACT.Sigmoid)
+
         offs_sb = load_list(offs, "offs_sb")
         for q in range(4):
             rows = x_scales[0, 4 * q : 4 * q + 4, :].bitcast(I32)
             nc.sync.dma_start(x_bytes[32 * q : 32 * (q + 1), :].bitcast(I32), rows.unsqueeze(0).broadcast_to([8, 4, T // 4]))
-        w1_raw = [load_weight(w1[:, :HALF], "w1_raw0")]
         two_sb = load_list(two, "two_sb")
-        w1_raw.append(load_weight(w1[:, HALF:], "w1_raw1"))
+        w1_raw = [load_weight(w1[:, HALF * c : HALF * (c + 1)], f"w1_raw{c}", f"raw{c}") for c in range(2)]
+        k1_sb = load_list(k1, "k1_sb")
+        nc.sync.dma_start(d_bytes[0:P:8, :].bitcast(I32), d_scales[0].bitcast(I32))
         x_table = load_words(x_words, "x_table")
-        n1_sb = load_list(n1, "n1_sb")
-        n2_sb = load_list(n2, "n2_sb")
-        d_table = load_words(d_words, "d_table")
-        n3_sb = load_list(n3, "n3_sb")
-        n4_sb = load_list(n4, "n4_sb")
         gain = keep.tile([P, PACK], F32, name="gain")
         nc.sync.dma_start(gain[:], gn.rearrange("(p t) o -> p (t o)", t=PACK))
-        w2_raw = load_weight(w2, "w2_raw")
+        d_table = load_words(d_words, "d_table")
+        n1_sb = load_list(n1, "n1_sb")
+        n2_sb = load_list(n2, "n2_sb")
+        n3_sb = load_list(n3, "n3_sb")
+        n4_sb = load_list(n4, "n4_sb")
         n5_sb = load_list(n5, "n5_sb")
 
         def gather_bytes(table, offsets, name):
-            picked = keep.tile([P, S], U8, name=name, align_bytes=64)
+            picked = keep.tile([P, S], U8, name=name, tag=name, align_bytes=64)
             nc.vector.tensor_copy(picked[:], table[:].indirect(offsets[:]))
             return picked
 
@@ -99,17 +101,18 @@ def tile_picked_twkeypathbghard_none_p_kernel(tc, x_words, x_scales, w1, d_words
             nc.tensor.matmul_mx(acc, lhsT=w_codes[:, cols].bitcast(FP8X4), lhsT_scale=w_scales[:, cols],
                                 rhs=codes[:].bitcast(FP8X4), rhs_scale=scales[:], start=True, stop=True)
 
+        xo_scales = gather_bytes(x_bytes, offs_sb, "xo_scales")
+        xt_scales = gather_bytes(x_bytes, two_sb, "xt_scales")
         dk_bytes = gather_bytes(d_bytes, k1_sb, "dk_bytes")
         dk_dealt = deal(dk_bytes, U8, "dk_dealt")
         for i in range(4):
-            nc.gpsimd.dma_start(dk_scales[i:P:32, :].bitcast(I32), dk_dealt[8 * i : P : 32, :].bitcast(I32))
-        xo_scales = gather_bytes(x_bytes, offs_sb, "xo_scales")
-        xt_scales = gather_bytes(x_bytes, two_sb, "xt_scales")
+            nc.sync.dma_start(dk_scales[i:P:32, :].bitcast(I32), dk_dealt[8 * i : P : 32, :].bitcast(I32))
 
         w1_bf = keep.tile([P, PACK * S], BF16, name="w1_bf", align_bytes=64)
         w1_dealt = w1_bf[:].rearrange("p (t m j) -> p m j t", t=PACK, j=PACK)
         for c in range(2):
             nc.scalar.copy(w1_dealt[:, 64 * c : 64 * (c + 1)], w1_raw[c][:].rearrange("p j (m t) -> p m j t", t=PACK))
+        w2_raw = load_weight(w2, "w2_raw", "dk_bytes")
         w1_codes, w1_scales = quantize(w1_bf[:], "w1")
         xo_codes = gather_words(x_table, offs_sb, "xo_codes")
         y_acc = [psum.tile([P, S], F32, name=f"y_acc{t}", tag=f"bank{t}") for t in range(PACK)]
@@ -123,52 +126,77 @@ def tile_picked_twkeypathbghard_none_p_kernel(tc, x_words, x_scales, w1, d_words
         for t in range(PACK):
             product(d_acc[t][:], dk_codes, dk_scales, t, xt_codes, xt_scales)
 
+        y_gain = keep.tile([P, PACK], F32, name="y_gain")
+        d_gain = keep.tile([P, PACK], F32, name="d_gain")
+        signs = keep.tile([P, HALF, PACK], BF16, name="signs")
+        nc.scalar.activation(y_gain[:], gain[:], ACT.Abs)
+        nc.scalar.activation(d_gain[:], gain[:], ACT.Abs, scale=0.0625)
+        nc.scalar.activation(signs[:], gain[:].unsqueeze(1).broadcast_to([P, HALF, PACK]), ACT.Sign)
+
         y_rows = [keep.tile([P, S], F32, name=f"y_rows{t}") for t in range(PACK)]
         d_rows = [keep.tile([P, S], F32, name=f"d_rows{t}") for t in range(PACK)]
-        w2_bf = keep.tile([P, PACK * S], BF16, name="w2_bf", align_bytes=64)
+        sums = [[keep.tile([P, PACK, HALF], F32, name=f"sums{c}{e}", tag=f"sums{c}{e}", align_bytes=64) for e in range(2)] for c in range(2)]
         h_acc = [psum.tile([P, S], F32, name=f"h_acc{m}", tag=f"bank{m}") for m in range(PACK)]
-        gain_b = gain[:].unsqueeze(1).unsqueeze(3).broadcast_to([P, HALF // 4, PACK, 4])
 
-        for c in range(S // HALF):
+        def add_picked(c, t):
             entries = slice(c * HALF // 16, (c + 1) * HALF // 16)
-            cols = slice(c * HALF, (c + 1) * HALF)
-            larger = keep.tile([P, PACK, HALF], F32, name=f"larger{c}")
-            for t in range(PACK):
-                if c == 0:
-                    nc.scalar.copy(y_rows[t][:], y_acc[t][:])
-                    if t == 0:
-                        nc.vector.tensor_scalar(d_rows[t][:], d_acc[t][:], 0.0625, None, ALU.mult)
-                    else:
-                        nc.scalar.activation(d_rows[t][:], d_acc[t][:], ACT.Copy, scale=0.0625)
-                sums = []
-                for y_list, d_list in ((n1_sb, n3_sb), (n2_sb, n4_sb)):
-                    y_picked = work.tile([P, HALF], F32, name="y_picked", bufs=16)
-                    nc.scalar.activation(y_picked[:], y_rows[t][:].indirect(y_list[:, entries]), ACT.Copy)
-                    total = work.tile([P, HALF], F32, name="total", bufs=4)
-                    nc.vector.tensor_tensor(total[:], d_rows[t][:].indirect(d_list[:, entries]), y_picked[:], ALU.add)
-                    sums.append(total)
-                nc.vector.tensor_tensor(larger[:, t, :], sums[0][:], sums[1][:], ALU.max)
-            if c == 0:
-                nc.scalar.copy(w2_bf[:].rearrange("p (c i j) -> p c j i", i=4, j=PACK), w2_raw[:].rearrange("p j (c i) -> p c j i", i=4))
-                w2_codes, w2_scales = quantize(w2_bf[:], "w2")
-            z_bf = keep.tile([P, PACK * HALF], BF16, name=f"z_bf{c}", align_bytes=64)
-            nc.vector.tensor_tensor(z_bf[:].rearrange("p (c i t) -> p c t i", i=4, t=PACK),
-                                    larger[:].rearrange("p t (c i) -> p c t i", i=4), gain_b, ALU.mult)
-            z_codes, z_scales = quantize(z_bf[:], f"z{c}")
-            for m in range(PACK):
-                product(h_acc[m][:, cols], w2_codes, w2_scales, m, z_codes, z_scales)
-                if c == 1 and m == 0:
-                    nc.vector.tensor_copy(h_rows[m][:, cols], h_acc[m][:, cols])
-                else:
-                    nc.scalar.copy(h_rows[m][:, cols], h_acc[m][:, cols])
+            for e, (y_list, d_list) in enumerate(((n1_sb, n3_sb), (n2_sb, n4_sb))):
+                y_picked = work.tile([P, HALF], F32, name="y_picked", bufs=4)
+                nc.scalar.activation(y_picked[:], y_rows[t][:].indirect(y_list[:, entries]), ACT.Copy)
+                nc.vector.tensor_tensor(sums[c][e][:, t, :], d_rows[t][:].indirect(d_list[:, entries]), y_picked[:], ALU.add)
 
+        def larger_sum(c):
+            unsigned = keep.tile([P, PACK * HALF], BF16, name=f"unsigned{c}")
+            first, second = [sums[c][e][:].rearrange("p t (c i) -> p c t i", i=4) for e in range(2)]
+            nc.vector.tensor_tensor(unsigned[:].rearrange("p (c i t) -> p c t i", i=4, t=PACK), first, second, ALU.max)
+            return unsigned
+
+        def signed(unsigned, c):
+            z_bf = keep.tile([P, PACK * HALF], BF16, name=f"z_bf{c}", align_bytes=64)
+            nc.vector.tensor_tensor(z_bf[:], unsigned[:], signs[:].rearrange("p c t -> p (c t)"), ALU.mult)
+            return z_bf
+
+        for t in range(PACK):
+            nc.scalar.activation(y_rows[t][:], y_acc[t][:], ACT.Copy, scale=y_gain[:, t : t + 1])
+            if t == 0:
+                nc.vector.tensor_scalar(d_rows[t][:], d_acc[t][:], d_gain[:, t : t + 1], None, ALU.mult)
+            else:
+                nc.scalar.activation(d_rows[t][:], d_acc[t][:], ACT.Copy, scale=d_gain[:, t : t + 1])
+            add_picked(0, t)
+        unsigned = larger_sum(0)
+        add_picked(1, 0)
+        z_bf = signed(unsigned, 0)
+        add_picked(1, 1)
+        z_codes, z_scales = quantize(z_bf[:], "z0")
+        w2_bf = keep.tile([P, PACK * S], BF16, name="w2_bf", tag="sums00", align_bytes=64)
+        nc.scalar.copy(w2_bf[:].rearrange("p (c i j) -> p c j i", i=4, j=PACK), w2_raw[:].rearrange("p j (c i) -> p c j i", i=4))
+        add_picked(1, 2)
+        w2_codes, w2_scales = quantize(w2_bf[:], "w2")
         for m in range(PACK):
+            product(h_acc[m][:, :HALF], w2_codes, w2_scales, m, z_codes, z_scales)
+        add_picked(1, 3)
+        for m in range(PACK):
+            nc.scalar.copy(h_rows[m][:, :HALF], h_acc[m][:, :HALF])
+        z_codes, z_scales = quantize(signed(larger_sum(1), 1)[:], "z1")
+        for m in range(PACK):
+            product(h_acc[m][:, HALF:], w2_codes, w2_scales, m, z_codes, z_scales)
+
+        def finish(m, cols, diff, gate):
+            result = keep.tile([P, HALF], F32, name=f"result{m}_{cols.start}")
+            nc.vector.tensor_tensor(result[:], diff[:], gate[:], ALU.mult)
+            nc.sync.dma_start(out[P * m : P * (m + 1), cols], result[:])
+
+        nc.vector.tensor_copy(h_rows[0][:, HALF:S], h_acc[0][:, HALF:])
+        waiting = None
+        for m in range(PACK):
+            if m + 1 < PACK:
+                nc.scalar.copy(h_rows[m + 1][:, HALF:S], h_acc[m + 1][:, HALF:])
             for c in range(S // HALF):
                 cols = slice(c * HALF, (c + 1) * HALF)
                 window = h_rows[m][:].indirect(n5_sb[:, c * 2 * HALF // 16 : (c + 1) * 2 * HALF // 16])
-                members = work.tile([P, HALF, 2], F32, name="members", bufs=4)
+                members = work.tile([P, HALF, 2], F32, name="members", bufs=3)
                 flat = members[:].rearrange("p c e -> p (c e)")
-                if (m, c) in ((0, 0), (2, 0)):
+                if (m, c) == (0, 0):
                     nc.vector.tensor_copy(flat, window)
                 else:
                     nc.scalar.activation(flat, window, ACT.Copy)
@@ -178,8 +206,9 @@ def tile_picked_twkeypathbghard_none_p_kernel(tc, x_words, x_scales, w1, d_words
                 nc.vector.tensor_tensor(lo[:], members[:, :, 0], members[:, :, 1], ALU.min)
                 gate = work.tile([P, HALF], F32, name="gate")
                 nc.scalar.activation(gate[:], hi[:], ACT.Sigmoid)
+                if waiting is not None:
+                    finish(*waiting)
                 diff = work.tile([P, HALF], F32, name="diff")
                 nc.vector.tensor_tensor(diff[:], h_rows[m][:, cols], lo[:], ALU.subtract)
-                result = work.tile([P, HALF], F32, name="result", bufs=8)
-                nc.vector.tensor_tensor(result[:], diff[:], gate[:], ALU.mult)
-                nc.sync.dma_start(out[P * m : P * (m + 1), cols], result[:])
+                waiting = (m, cols, diff, gate)
+        finish(*waiting)

@@ -35,7 +35,7 @@ def tile_picked_twkeypathbghard_none_p_kernel(tc, x_words, x_scales, w1, d_words
             return tile
 
         def load_words(src, name):
-            tile = keep.tile([P, T], I32, name=name)
+            tile = keep.tile([P, T], I32, name=name, tag=name, align_bytes=64)
             nc.sync.dma_start(tile[:], src[0].rearrange("p n t -> p (n t)").bitcast(I32))
             return tile
 
@@ -64,12 +64,12 @@ def tile_picked_twkeypathbghard_none_p_kernel(tc, x_words, x_scales, w1, d_words
         w1_raw = [load_weight(w1[:, HALF * c : HALF * (c + 1)], f"w1_raw{c}", f"raw{c}") for c in range(2)]
         k1_sb = load_list(k1, "k1_sb")
         nc.sync.dma_start(d_bytes[0:P:8, :].bitcast(I32), d_scales[0].bitcast(I32))
-        x_table = load_words(x_words, "x_table")
         gain = keep.tile([P, PACK], F32, name="gain")
         nc.sync.dma_start(gain[:], gn.rearrange("(p t) o -> p (t o)", t=PACK))
-        d_table = load_words(d_words, "d_table")
+        x_table = load_words(x_words, "x_table")
         n1_sb = load_list(n1, "n1_sb")
         n2_sb = load_list(n2, "n2_sb")
+        d_table = load_words(d_words, "d_table")
         n3_sb = load_list(n3, "n3_sb")
         n4_sb = load_list(n4, "n4_sb")
         n5_sb = load_list(n5, "n5_sb")
@@ -80,7 +80,7 @@ def tile_picked_twkeypathbghard_none_p_kernel(tc, x_words, x_scales, w1, d_words
             return picked
 
         def gather_words(table, offsets, name):
-            picked = keep.tile([P, S], U32, name=name, align_bytes=64)
+            picked = keep.tile([P, S], U32, name=name, tag=name, align_bytes=64)
             nc.vector.tensor_copy(picked[:], table[:].bitcast(U32).indirect(offsets[:]))
             return picked
 
@@ -133,21 +133,22 @@ def tile_picked_twkeypathbghard_none_p_kernel(tc, x_words, x_scales, w1, d_words
         nc.scalar.activation(d_gain[:], gain[:], ACT.Abs, scale=0.0625)
         nc.scalar.activation(signs[:], gain[:].unsqueeze(1).broadcast_to([P, HALF, PACK]), ACT.Sign)
 
-        y_rows = [keep.tile([P, S], F32, name=f"y_rows{t}") for t in range(PACK)]
-        d_rows = [keep.tile([P, S], F32, name=f"d_rows{t}") for t in range(PACK)]
-        sums = [[keep.tile([P, PACK, HALF], F32, name=f"sums{c}{e}", tag=f"sums{c}{e}", align_bytes=64) for e in range(2)] for c in range(2)]
+        y_tags = ["y_rows0", "y_rows1", "dk_words", "d_table"]
+        y_rows = [keep.tile([P, S], F32, name=f"y_rows{t}", tag=y_tags[t], align_bytes=64) for t in range(PACK)]
+        d_rows = [keep.tile([P, S], F32, name=f"d_rows{t}", tag=f"d_rows{t}", align_bytes=64) for t in range(PACK)]
+        sums = [keep.tile([P, PACK, S], F32, name=f"sums{e}") for e in range(2)]
         h_acc = [psum.tile([P, S], F32, name=f"h_acc{m}", tag=f"bank{m}") for m in range(PACK)]
+        halves = [slice(0, HALF), slice(HALF, S)]
 
-        def add_picked(c, t):
-            entries = slice(c * HALF // 16, (c + 1) * HALF // 16)
-            for e, (y_list, d_list) in enumerate(((n1_sb, n3_sb), (n2_sb, n4_sb))):
-                y_picked = work.tile([P, HALF], F32, name="y_picked", bufs=4)
-                nc.scalar.activation(y_picked[:], y_rows[t][:].indirect(y_list[:, entries]), ACT.Copy)
-                nc.vector.tensor_tensor(sums[c][e][:, t, :], d_rows[t][:].indirect(d_list[:, entries]), y_picked[:], ALU.add)
+        def empty_bank(on_vector, rows, acc, factor):
+            if on_vector:
+                nc.vector.tensor_scalar(rows[:], acc[:], factor, None, ALU.mult)
+            else:
+                nc.scalar.activation(rows[:], acc[:], ACT.Copy, scale=factor)
 
         def larger_sum(c):
             unsigned = keep.tile([P, PACK * HALF], BF16, name=f"unsigned{c}")
-            first, second = [sums[c][e][:].rearrange("p t (c i) -> p c t i", i=4) for e in range(2)]
+            first, second = [sums[e][:, :, halves[c]].rearrange("p t (c i) -> p c t i", i=4) for e in range(2)]
             nc.vector.tensor_tensor(unsigned[:].rearrange("p (c i t) -> p c t i", i=4, t=PACK), first, second, ALU.max)
             return unsigned
 
@@ -156,28 +157,29 @@ def tile_picked_twkeypathbghard_none_p_kernel(tc, x_words, x_scales, w1, d_words
             nc.vector.tensor_tensor(z_bf[:], unsigned[:], signs[:].rearrange("p c t -> p (c t)"), ALU.mult)
             return z_bf
 
+        for t in (2, 3):
+            empty_bank(True, y_rows[t], y_acc[t], y_gain[:, t : t + 1])
         for t in range(PACK):
-            nc.scalar.activation(y_rows[t][:], y_acc[t][:], ACT.Copy, scale=y_gain[:, t : t + 1])
-            if t == 0:
-                nc.vector.tensor_scalar(d_rows[t][:], d_acc[t][:], d_gain[:, t : t + 1], None, ALU.mult)
-            else:
-                nc.scalar.activation(d_rows[t][:], d_acc[t][:], ACT.Copy, scale=d_gain[:, t : t + 1])
-            add_picked(0, t)
-        unsigned = larger_sum(0)
-        add_picked(1, 0)
-        z_bf = signed(unsigned, 0)
-        add_picked(1, 1)
-        z_codes, z_scales = quantize(z_bf[:], "z0")
-        w2_bf = keep.tile([P, PACK * S], BF16, name="w2_bf", tag="sums00", align_bytes=64)
+            if t not in (2, 3):
+                empty_bank(False, y_rows[t], y_acc[t], y_gain[:, t : t + 1])
+            empty_bank(t == 0, d_rows[t], d_acc[t], d_gain[:, t : t + 1])
+            for cols in halves:
+                entries = slice(cols.start // 16, cols.stop // 16)
+                for e, (y_list, d_list) in enumerate(((n1_sb, n3_sb), (n2_sb, n4_sb))):
+                    y_picked = work.tile([P, HALF], F32, name="y_picked", bufs=6)
+                    nc.scalar.activation(y_picked[:], y_rows[t][:].indirect(y_list[:, entries]), ACT.Copy)
+                    nc.vector.tensor_tensor(sums[e][:, t, cols], d_rows[t][:].indirect(d_list[:, entries]), y_picked[:], ALU.add)
+        unsigned = [larger_sum(0)]
+        w2_bf = keep.tile([P, PACK * S], BF16, name="w2_bf", tag="d_rows2", align_bytes=64)
         nc.scalar.copy(w2_bf[:].rearrange("p (c i j) -> p c j i", i=4, j=PACK), w2_raw[:].rearrange("p j (c i) -> p c j i", i=4))
-        add_picked(1, 2)
+        unsigned.append(larger_sum(1))
+        z_bf = signed(unsigned[0], 0)
         w2_codes, w2_scales = quantize(w2_bf[:], "w2")
+        z_codes, z_scales = quantize(z_bf[:], "z0")
         for m in range(PACK):
             product(h_acc[m][:, :HALF], w2_codes, w2_scales, m, z_codes, z_scales)
-        add_picked(1, 3)
-        for m in range(PACK):
             nc.scalar.copy(h_rows[m][:, :HALF], h_acc[m][:, :HALF])
-        z_codes, z_scales = quantize(signed(larger_sum(1), 1)[:], "z1")
+        z_codes, z_scales = quantize(signed(unsigned[1], 1)[:], "z1")
         for m in range(PACK):
             product(h_acc[m][:, HALF:], w2_codes, w2_scales, m, z_codes, z_scales)
 
@@ -187,28 +189,28 @@ def tile_picked_twkeypathbghard_none_p_kernel(tc, x_words, x_scales, w1, d_words
             nc.sync.dma_start(out[P * m : P * (m + 1), cols], result[:])
 
         nc.vector.tensor_copy(h_rows[0][:, HALF:S], h_acc[0][:, HALF:])
-        waiting = None
+        waiting = []
         for m in range(PACK):
             if m + 1 < PACK:
                 nc.scalar.copy(h_rows[m + 1][:, HALF:S], h_acc[m + 1][:, HALF:])
-            for c in range(S // HALF):
-                cols = slice(c * HALF, (c + 1) * HALF)
-                window = h_rows[m][:].indirect(n5_sb[:, c * 2 * HALF // 16 : (c + 1) * 2 * HALF // 16])
+            for c, cols in enumerate(halves):
+                window = h_rows[m][:].indirect(n5_sb[:, cols.start // 8 : cols.stop // 8])
                 members = work.tile([P, HALF, 2], F32, name="members", bufs=3)
                 flat = members[:].rearrange("p c e -> p (c e)")
-                if (m, c) == (0, 0):
+                if (m, c) in ((0, 0), (1, 1)):
                     nc.vector.tensor_copy(flat, window)
                 else:
                     nc.scalar.activation(flat, window, ACT.Copy)
-                hi = work.tile([P, HALF], F32, name="hi")
-                lo = work.tile([P, HALF], F32, name="lo")
+                hi = keep.tile([P, HALF], F32, name=f"hi{m}{c}")
+                lo = keep.tile([P, HALF], F32, name=f"lo{m}{c}")
+                gate = keep.tile([P, HALF], F32, name=f"gate{m}{c}")
+                diff = keep.tile([P, HALF], F32, name=f"diff{m}{c}")
                 nc.vector.tensor_tensor(hi[:], members[:, :, 0], members[:, :, 1], ALU.max)
                 nc.vector.tensor_tensor(lo[:], members[:, :, 0], members[:, :, 1], ALU.min)
-                gate = work.tile([P, HALF], F32, name="gate")
                 nc.scalar.activation(gate[:], hi[:], ACT.Sigmoid)
-                if waiting is not None:
-                    finish(*waiting)
-                diff = work.tile([P, HALF], F32, name="diff")
+                if len(waiting) == 2:
+                    finish(*waiting.pop(0))
                 nc.vector.tensor_tensor(diff[:], h_rows[m][:, cols], lo[:], ALU.subtract)
-                waiting = (m, cols, diff, gate)
-        finish(*waiting)
+                waiting.append((m, cols, diff, gate))
+        for item in waiting:
+            finish(*item)

@@ -162,20 +162,26 @@ def tile_picked_twkeypathbghard_none_p_kernel(tc, x_words, x_scales, w1, d_words
         for t in range(PACK):
             if t not in (2, 3):
                 empty_bank(False, y_rows[t], y_acc[t], y_gain[:, t : t + 1])
-            empty_bank(t == 0, d_rows[t], d_acc[t], d_gain[:, t : t + 1])
-            for cols in halves:
+            empty_bank(t < 2, d_rows[t], d_acc[t], d_gain[:, t : t + 1])
+            for c, cols in enumerate(halves):
+                if (t, c) == (PACK - 1, 1):
+                    unsigned = [larger_sum(0)]
                 entries = slice(cols.start // 16, cols.stop // 16)
                 for e, (y_list, d_list) in enumerate(((n1_sb, n3_sb), (n2_sb, n4_sb))):
-                    y_picked = work.tile([P, HALF], F32, name="y_picked", bufs=6)
+                    y_picked = work.tile([P, HALF], F32, name="y_picked", tag="picked", bufs=6)
                     nc.scalar.activation(y_picked[:], y_rows[t][:].indirect(y_list[:, entries]), ACT.Copy)
-                    nc.vector.tensor_tensor(sums[e][:, t, cols], d_rows[t][:].indirect(d_list[:, entries]), y_picked[:], ALU.add)
-        unsigned = [larger_sum(0)]
+                    d_picked = d_rows[t][:].indirect(d_list[:, entries])
+                    if t > 0 and c == 1 and e == 1:
+                        d_plain = work.tile([P, HALF], F32, name="d_plain", tag="picked", bufs=6)
+                        nc.scalar.activation(d_plain[:], d_picked, ACT.Copy)
+                        d_picked = d_plain[:]
+                    nc.vector.tensor_tensor(sums[e][:, t, cols], d_picked, y_picked[:], ALU.add)
         w2_bf = keep.tile([P, PACK * S], BF16, name="w2_bf", tag="d_rows2", align_bytes=64)
         nc.scalar.copy(w2_bf[:].rearrange("p (c i j) -> p c j i", i=4, j=PACK), w2_raw[:].rearrange("p j (c i) -> p c j i", i=4))
-        unsigned.append(larger_sum(1))
         z_bf = signed(unsigned[0], 0)
-        w2_codes, w2_scales = quantize(w2_bf[:], "w2")
+        unsigned.append(larger_sum(1))
         z_codes, z_scales = quantize(z_bf[:], "z0")
+        w2_codes, w2_scales = quantize(w2_bf[:], "w2")
         for m in range(PACK):
             product(h_acc[m][:, :HALF], w2_codes, w2_scales, m, z_codes, z_scales)
             nc.scalar.copy(h_rows[m][:, :HALF], h_acc[m][:, :HALF])

@@ -171,7 +171,7 @@ def tile_picked_twkeypathbghard_none_p_kernel(tc, x_words, x_scales, w1, d_words
                     y_picked = work.tile([P, HALF], F32, name="y_picked", tag="picked", bufs=6)
                     nc.scalar.activation(y_picked[:], y_rows[t][:].indirect(y_list[:, entries]), ACT.Copy)
                     d_picked = d_rows[t][:].indirect(d_list[:, entries])
-                    if t > 0 and c == 1 and e == 1:
+                    if c == 1 and 2 * t + e >= 5:
                         d_plain = work.tile([P, HALF], F32, name="d_plain", tag="picked", bufs=6)
                         nc.scalar.activation(d_plain[:], d_picked, ACT.Copy)
                         d_picked = d_plain[:]
@@ -197,16 +197,19 @@ def tile_picked_twkeypathbghard_none_p_kernel(tc, x_words, x_scales, w1, d_words
         nc.vector.tensor_copy(h_rows[0][:, HALF:S], h_acc[0][:, HALF:])
         waiting = []
         for m in range(PACK):
-            if m + 1 < PACK:
+            if m == 1:
+                nc.vector.tensor_copy(h_rows[m + 1][:, HALF:S], h_acc[m + 1][:, HALF:])
+            elif m + 1 < PACK:
                 nc.scalar.copy(h_rows[m + 1][:, HALF:S], h_acc[m + 1][:, HALF:])
             for c, cols in enumerate(halves):
-                window = h_rows[m][:].indirect(n5_sb[:, cols.start // 8 : cols.stop // 8])
+                entries = n5_sb[:, cols.start // 8 : cols.stop // 8]
                 members = work.tile([P, HALF, 2], F32, name="members", bufs=3)
                 flat = members[:].rearrange("p c e -> p (c e)")
-                if (m, c) in ((0, 0), (1, 1)):
-                    nc.vector.tensor_copy(flat, window)
-                else:
-                    nc.scalar.activation(flat, window, ACT.Copy)
+                on_vector = {(0, 0): 2 * HALF, (1, 1): HALF}.get((m, c), 0)
+                if on_vector > 0:
+                    nc.vector.tensor_copy(flat[:, :on_vector], h_rows[m][:].indirect(entries[:, : on_vector // 16]))
+                if on_vector < 2 * HALF:
+                    nc.scalar.activation(flat[:, on_vector:], h_rows[m][:].indirect(entries[:, on_vector // 16 :]), ACT.Copy)
                 hi = keep.tile([P, HALF], F32, name=f"hi{m}{c}")
                 lo = keep.tile([P, HALF], F32, name=f"lo{m}{c}")
                 gate = keep.tile([P, HALF], F32, name=f"gate{m}{c}")

from contextlib import ExitStack

import concourse.mybir as mybir

F32 = mybir.dt.float32
BF16 = mybir.dt.bfloat16
I32 = mybir.dt.int32
U32 = mybir.dt.uint32
U16 = mybir.dt.uint16
U8 = mybir.dt.uint8
FP8X4 = mybir.dt.float8_e4m3fn_x4
ALU = mybir.AluOpType
ACT = mybir.ActivationFunctionType

P = 128
PACK = 4
T = 2048
S = 512
HALF = 256
SPARE = 32
FLOPS = 3 * 2 * 512 * 512 * 512


def tile_picked_twkeypathbghard_none_p_kernel(tc, x_words, x_scales, w1, d_words, d_scales, gn, w2, offs, k1, two, n1, n2, n3, n4, n5, out):
    nc = tc.nc
    with ExitStack() as ctx:
        lists = ctx.enter_context(tc.tile_pool(name="lists", bufs=1))
        keep = ctx.enter_context(tc.tile_pool(name="keep", bufs=1))
        work = ctx.enter_context(tc.tile_pool(name="work", bufs=3))
        psum = ctx.enter_context(tc.psum_pool(name="psum", bufs=1))

        def load_list(src, name):
            tile = lists.tile(list(src.shape), U16, name=name)
            nc.sync.dma_start(tile[:], src)
            return tile

        def load_words(src, name):
            tile = keep.tile([P, T], I32, name=name, tag=name, align_bytes=64)
            nc.sync.dma_start(tile[:], src[0].rearrange("p n t -> p (n t)").bitcast(I32))
            return tile

        def load_weight(src, name, tag):
            tile = keep.tile([P, PACK, src.shape[1]], F32, name=name, tag=tag, align_bytes=64)
            nc.sync.dma_start(tile[:], src.rearrange("(p j) c -> p j c", j=PACK))
            return tile

        d_bytes = keep.tile([P, T], U8, name="d_bytes")
        x_bytes = keep.tile([P, T], U8, name="x_bytes")
        nc.gpsimd.memset(d_bytes[:].bitcast(I32), 0)
        dk_scales = keep.tile([P, S], U8, name="dk_scales", align_bytes=64)
        nc.gpsimd.memset(dk_scales[:].bitcast(I32), 0)
        h_rows = [keep.tile([P, S + SPARE], F32, name=f"h_rows{m}") for m in range(PACK)]
        for m in range(PACK):
            nc.gpsimd.memset(h_rows[m][:, S:], 0.0)

        warm = keep.tile([P, 8], F32, name="warm")
        nc.scalar.activation(warm[:], h_rows[0][:, S : S + 8], ACT.Sigmoid)

        offs_sb = load_list(offs, "offs_sb")
        for q in range(4):
            rows = x_scales[0, 4 * q : 4 * q + 4, :].bitcast(I32)
            nc.sync.dma_start(x_bytes[32 * q : 32 * (q + 1), :].bitcast(I32), rows.unsqueeze(0).broadcast_to([8, 4, T // 4]))
        two_sb = load_list(two, "two_sb")
        w1_raw = [load_weight(w1[:, HALF * c : HALF * (c + 1)], f"w1_raw{c}", f"raw{c}") for c in range(2)]
        k1_sb = load_list(k1, "k1_sb")
        nc.sync.dma_start(d_bytes[0:P:8, :].bitcast(I32), d_scales[0].bitcast(I32))
        gain = keep.tile([P, PACK], F32, name="gain")
        nc.sync.dma_start(gain[:], gn.rearrange("(p t) o -> p (t o)", t=PACK))
        x_table = load_words(x_words, "x_table")
        n1_sb = load_list(n1, "n1_sb")
        n2_sb = load_list(n2, "n2_sb")
        d_table = load_words(d_words, "d_table")
        n3_sb = load_list(n3, "n3_sb")
        n4_sb = load_list(n4, "n4_sb")
        n5_sb = load_list(n5, "n5_sb")

        def gather_bytes(table, offsets, name):
            picked = keep.tile([P, S], U8, name=name, tag=name, align_bytes=64)
            nc.vector.tensor_copy(picked[:], table[:].indirect(offsets[:]))
            return picked

        def gather_words(table, offsets, name):
            picked = keep.tile([P, S], U32, name=name, tag=name, align_bytes=64)
            nc.vector.tensor_copy(picked[:], table[:].bitcast(U32).indirect(offsets[:]))
            return picked

        def deal(src, dtype, name):
            dealt = keep.tile([P, S], dtype, name=name, align_bytes=64)
            nc.vector.tensor_copy(dealt[:].rearrange("p (t m) -> p m t", t=PACK), src[:].rearrange("p (m t) -> p m t", t=PACK))
            return dealt

        def quantize(values, name):
            width = values.shape[1] // PACK
            codes = keep.tile([P, width], U32, name=name + "_codes", align_bytes=64)
            scales = keep.tile([P, width], U8, name=name + "_scales", align_bytes=64)
            nc.vector.quantize_mx(out=codes[:].bitcast(FP8X4), scales=scales[:], in_=values)
            return codes, scales

        def product(acc, w_codes, w_scales, t, codes, scales):
            cols = slice(P * t, P * (t + 1))
            nc.tensor.matmul_mx(acc, lhsT=w_codes[:, cols].bitcast(FP8X4), lhsT_scale=w_scales[:, cols],
                                rhs=codes[:].bitcast(FP8X4), rhs_scale=scales[:], start=True, stop=True)

        xo_scales = gather_bytes(x_bytes, offs_sb, "xo_scales")
        xt_scales = gather_bytes(x_bytes, two_sb, "xt_scales")
        dk_bytes = gather_bytes(d_bytes, k1_sb, "dk_bytes")
        dk_dealt = deal(dk_bytes, U8, "dk_dealt")
        for i in range(4):
            nc.sync.dma_start(dk_scales[i:P:32, :].bitcast(I32), dk_dealt[8 * i : P : 32, :].bitcast(I32))

        w1_bf = keep.tile([P, PACK * S], BF16, name="w1_bf", align_bytes=64)
        w1_dealt = w1_bf[:].rearrange("p (t m j) -> p m j t", t=PACK, j=PACK)
        for c in range(2):
            nc.scalar.copy(w1_dealt[:, 64 * c : 64 * (c + 1)], w1_raw[c][:].rearrange("p j (m t) -> p m j t", t=PACK))
        w2_raw = load_weight(w2, "w2_raw", "dk_bytes")
        w1_codes, w1_scales = quantize(w1_bf[:], "w1")
        xo_codes = gather_words(x_table, offs_sb, "xo_codes")
        y_acc = [psum.tile([P, S], F32, name=f"y_acc{t}", tag=f"bank{t}") for t in range(PACK)]
        for t in range(PACK):
            product(y_acc[t][:], w1_codes, w1_scales, t, xo_codes, xo_scales)

        xt_codes = gather_words(x_table, two_sb, "xt_codes")
        dk_words = gather_words(d_table, k1_sb, "dk_words")
        dk_codes = deal(dk_words, U32, "dk_codes")
        d_acc = [psum.tile([P, S], F32, name=f"d_acc{t}", tag=f"bank{PACK + t}") for t in range(PACK)]
        for t in range(PACK):
            product(d_acc[t][:], dk_codes, dk_scales, t, xt_codes, xt_scales)

        y_gain = keep.tile([P, PACK], F32, name="y_gain")
        d_gain = keep.tile([P, PACK], F32, name="d_gain")
        signs = keep.tile([P, HALF, PACK], BF16, name="signs")
        nc.scalar.activation(y_gain[:], gain[:], ACT.Abs)
        nc.scalar.activation(d_gain[:], gain[:], ACT.Abs, scale=0.0625)
        nc.scalar.activation(signs[:], gain[:].unsqueeze(1).broadcast_to([P, HALF, PACK]), ACT.Sign)

        y_tags = ["y_rows0", "y_rows1", "dk_words", "d_table"]
        y_rows = [keep.tile([P, S], F32, name=f"y_rows{t}", tag=y_tags[t], align_bytes=64) for t in range(PACK)]
        d_rows = [keep.tile([P, S], F32, name=f"d_rows{t}", tag=f"d_rows{t}", align_bytes=64) for t in range(PACK)]
        sums = [keep.tile([P, PACK, S], F32, name=f"sums{e}") for e in range(2)]
        h_acc = [psum.tile([P, S], F32, name=f"h_acc{m}", tag=f"bank{m}") for m in range(PACK)]
        halves = [slice(0, HALF), slice(HALF, S)]

        def empty_bank(on_vector, rows, acc, factor):
            if on_vector:
                nc.vector.tensor_scalar(rows[:], acc[:], factor, None, ALU.mult)
            else:
                nc.scalar.activation(rows[:], acc[:], ACT.Copy, scale=factor)

        def larger_sum(c):
            unsigned = keep.tile([P, PACK * HALF], BF16, name=f"unsigned{c}")
            first, second = [sums[e][:, :, halves[c]].rearrange("p t (c i) -> p c t i", i=4) for e in range(2)]
            nc.vector.tensor_tensor(unsigned[:].rearrange("p (c i t) -> p c t i", i=4, t=PACK), first, second, ALU.max)
            return unsigned

        def signed(unsigned, c):
            z_bf = keep.tile([P, PACK * HALF], BF16, name=f"z_bf{c}", align_bytes=64)
            nc.vector.tensor_tensor(z_bf[:], unsigned[:], signs[:].rearrange("p c t -> p (c t)"), ALU.mult)
            return z_bf

        for t in (2, 3):
            empty_bank(True, y_rows[t], y_acc[t], y_gain[:, t : t + 1])
        for t in range(PACK):
            if t not in (2, 3):
                empty_bank(False, y_rows[t], y_acc[t], y_gain[:, t : t + 1])
            empty_bank(t < 2, d_rows[t], d_acc[t], d_gain[:, t : t + 1])
            for c, cols in enumerate(halves):
                if (t, c) == (PACK - 1, 1):
                    unsigned = [larger_sum(0)]
                entries = slice(cols.start // 16, cols.stop // 16)
                for e, (y_list, d_list) in enumerate(((n1_sb, n3_sb), (n2_sb, n4_sb))):
                    y_picked = work.tile([P, HALF], F32, name="y_picked", tag="picked", bufs=6)
                    nc.scalar.activation(y_picked[:], y_rows[t][:].indirect(y_list[:, entries]), ACT.Copy)
                    d_picked = d_rows[t][:].indirect(d_list[:, entries])
                    if c == 1 and 2 * t + e >= 5:
                        d_plain = work.tile([P, HALF], F32, name="d_plain", tag="picked", bufs=6)
                        nc.scalar.activation(d_plain[:], d_picked, ACT.Copy)
                        d_picked = d_plain[:]
                    nc.vector.tensor_tensor(sums[e][:, t, cols], d_picked, y_picked[:], ALU.add)
        w2_bf = keep.tile([P, PACK * S], BF16, name="w2_bf", tag="d_rows2", align_bytes=64)
        nc.scalar.copy(w2_bf[:].rearrange("p (c i j) -> p c j i", i=4, j=PACK), w2_raw[:].rearrange("p j (c i) -> p c j i", i=4))
        z_bf = signed(unsigned[0], 0)
        unsigned.append(larger_sum(1))
        z_codes, z_scales = quantize(z_bf[:], "z0")
        w2_codes, w2_scales = quantize(w2_bf[:], "w2")
        for m in range(PACK):
            product(h_acc[m][:, :HALF], w2_codes, w2_scales, m, z_codes, z_scales)
            nc.scalar.copy(h_rows[m][:, :HALF], h_acc[m][:, :HALF])
        z_codes, z_scales = quantize(signed(unsigned[1], 1)[:], "z1")
        for m in range(PACK):
            product(h_acc[m][:, HALF:], w2_codes, w2_scales, m, z_codes, z_scales)

        def finish(m, cols, diff, gate):
            result = keep.tile([P, HALF], F32, name=f"result{m}_{cols.start}")
            nc.vector.tensor_tensor(result[:], diff[:], gate[:], ALU.mult)
            nc.sync.dma_start(out[P * m : P * (m + 1), cols], result[:])

        nc.vector.tensor_copy(h_rows[0][:, HALF:S], h_acc[0][:, HALF:])
        waiting = []
        for m in range(PACK):
            if m == 1:
                nc.vector.tensor_copy(h_rows[m + 1][:, HALF:S], h_acc[m + 1][:, HALF:])
            elif m + 1 < PACK:
                nc.scalar.copy(h_rows[m + 1][:, HALF:S], h_acc[m + 1][:, HALF:])
            for c, cols in enumerate(halves):
                entries = n5_sb[:, cols.start // 8 : cols.stop // 8]
                members = work.tile([P, HALF, 2], F32, name="members", bufs=3)
                flat = members[:].rearrange("p c e -> p (c e)")
                on_vector = {(0, 0): 2 * HALF, (1, 1): HALF}.get((m, c), 0)
                if on_vector > 0:
                    nc.vector.tensor_copy(flat[:, :on_vector], h_rows[m][:].indirect(entries[:, : on_vector // 16]))
                if on_vector < 2 * HALF:
                    nc.scalar.activation(flat[:, on_vector:], h_rows[m][:].indirect(entries[:, on_vector // 16 :]), ACT.Copy)
                hi = keep.tile([P, HALF], F32, name=f"hi{m}{c}")
                lo = keep.tile([P, HALF], F32, name=f"lo{m}{c}")
                gate = keep.tile([P, HALF], F32, name=f"gate{m}{c}")
                diff = keep.tile([P, HALF], F32, name=f"diff{m}{c}")
                nc.vector.tensor_tensor(hi[:], members[:, :, 0], members[:, :, 1], ALU.max)
                nc.vector.tensor_tensor(lo[:], members[:, :, 0], members[:, :, 1], ALU.min)
                nc.scalar.activation(gate[:], hi[:], ACT.Sigmoid)
                if len(waiting) == 2:
                    finish(*waiting.pop(0))
                nc.vector.tensor_tensor(diff[:], h_rows[m][:, cols], lo[:], ALU.subtract)
                waiting.append((m, cols, diff, gate))
        for item in waiting:
            finish(*item)
